import numpy as np
import ml_dtypes


def mxq(x, axis, fmt="e4m3"):
    dtype, down = {"e4m3": (ml_dtypes.float8_e4m3fn, 7), "e5m2": (ml_dtypes.float8_e5m2, 14)}[fmt]
    v = np.moveaxis(np.asarray(x, np.float32).astype(ml_dtypes.bfloat16).astype(np.float64), axis, -1)
    blocks = v.reshape(v.shape[:-1] + (-1, 32))
    amax = np.abs(blocks).max(-1, keepdims=True)
    byte = np.maximum(np.where(amax > 0, np.frexp(amax)[1] - 1 + 127, 0) - down, 1)
    scale = np.exp2(byte - 127.0)
    codes = (blocks / scale).astype(np.float32).astype(dtype).astype(np.float64)
    return np.moveaxis((codes * scale).reshape(v.shape), -1, axis)


WIDE = False


def mx_kscale(k):
    if not WIDE:
        return np.ones(k)
    levels = np.array([10, -10, 5, -5, 0])
    if k % 512:
        return np.exp2(np.random.permutation(np.resize(levels, k // 32))).repeat(32)
    a = np.empty((k // 512, 16))
    for p in range(k // 512):
        a[p, :8] = np.random.permutation(np.resize(levels, 8))
        for g in range(8):
            far = levels[np.abs(levels - a[p, g]) >= 10]
            a[p, g + 8] = far[np.random.randint(len(far))]
    return np.exp2(a.ravel()).repeat(32)


def f64(x):
    return np.asarray(x).astype(np.float64)


def striped(idx):
    return np.tile(idx.reshape(-1, 16).T, (8, 1)).astype(np.uint16)


def unstriped(offs):
    return offs[:16].T.reshape(-1).astype(np.int64)


def sigmoid(v):
    return 1.0 / (1.0 + np.exp(-np.maximum(v, -700.0)))


K, T, E, H, N = 1024, 768, 6, 512, 128
COUNTS = (128, 128, 128, 384, 384, 384)
STARTS = np.cumsum((0,) + COUNTS)


def by_expert(wq, xq):
    return np.concatenate([wq[e].T @ xq[:, STARTS[e]:STARTS[e + 1]] for e in range(E)], axis=1)


def setup_inputs():
    n = np.random.standard_normal
    s = mx_kscale(K)[:, None]
    u = mx_kscale(H)
    both = np.repeat(np.arange(E), COUNTS)
    pair = np.stack([both[:T], both[T:]])[:, np.random.permutation(T)]
    pair = np.where(np.random.rand(T) < 0.5, pair, pair[::-1])
    order = np.argsort(pair.reshape(-1), kind="stable")
    slot_token = order % T; pos = np.empty(2 * T, np.int64); pos[order] = np.arange(2 * T); pos = pos.reshape(2, T)
    g = np.random.uniform(0.2, 0.8, T)
    return {
        "xT": (n((K, T)) * s).astype(np.float32),
        "w1": (n((E, K, H)) / np.sqrt(K) / s[None]).astype(np.float32),
        "w3": (n((E, K, H)) / np.sqrt(K) / s[None] * u[None, None, :]).astype(np.float32),
        "w2": (n((E, H, N)) / np.sqrt(H) / u[None, :, None]).astype(np.float32),
        "gate": np.stack([np.tile(g, (N, 1)), np.tile(1.0 - g, (N, 1))]).astype(np.float32),
        "offs": striped(slot_token),
        "pos1": striped(pos[0]),
        "pos2": striped(pos[1]),
    }


def reference(xT, w1, w3, w2, gate, offs, pos1, pos2):
    idx = unstriped(offs)
    xq = mxq(f64(xT)[:, idx], 0, "e4m3")
    h = sigmoid(by_expert(mxq(f64(w1), 1, "e4m3"), xq))
    h = h * by_expert(mxq(f64(w3), 1, "e4m3"), xq)
    y = by_expert(mxq(f64(w2), 1, "e4m3"), mxq(h, 0, "e4m3"))
    return f64(gate[0]) * y[:, unstriped(pos1)] + f64(gate[1]) * y[:, unstriped(pos2)]

@@ -1,0 +1,271 @@
+from contextlib import ExitStack
+
+import concourse.mybir as mybir
+
+T, E, H, N = 768, 6, 512, 128
+SLOTS = 1536
+STARTS = (0, 128, 256, 384, 768, 1152)
+COUNTS = (128, 128, 128, 384, 384, 384)
+ORDER = (3, 0, 4, 1, 5, 2)
+FLOPS = 3422552064
+
+P = 128
+J = 4
+K_PASS = 512
+PASSES = 2
+PIECE = 384
+UNIT = 128
+AHEAD = 9
+
+F32 = mybir.dt.float32
+BF16 = mybir.dt.bfloat16
+U32 = mybir.dt.uint32
+U16 = mybir.dt.uint16
+U8 = mybir.dt.uint8
+FP8X4 = mybir.dt.float8_e4m3fn_x4
+MULT = mybir.AluOpType.mult
+ADD = mybir.AluOpType.add
+SIGMOID = mybir.ActivationFunctionType.Sigmoid
+
+
+def tile_moe_rag_glu_sigmoid_kernel(tc, xT, w1, w3, w2, gate, offs, pos1, pos2, out):
+    nc = tc.nc
+    with ExitStack() as ctx:
+        lists = ctx.enter_context(tc.tile_pool(name="lists", bufs=1))
+        keep = ctx.enter_context(tc.tile_pool(name="keep", bufs=1))
+        raws = ctx.enter_context(tc.tile_pool(name="raws", bufs=11))
+        raws2 = ctx.enter_context(tc.tile_pool(name="raws2", bufs=3))
+        grps = ctx.enter_context(tc.tile_pool(name="grps", bufs=4))
+        codes = ctx.enter_context(tc.tile_pool(name="codes", bufs=3))
+        hid = ctx.enter_context(tc.tile_pool(name="hid", bufs=6))
+        psum_a = ctx.enter_context(tc.psum_pool(name="psum_a", bufs=3))
+        psum_g = ctx.enter_context(tc.psum_pool(name="psum_g", bufs=3))
+        psum_y = ctx.enter_context(tc.psum_pool(name="psum_y", bufs=2))
+
+        offs_t = lists.tile([P, SLOTS // 16], U16, name="offs_t")
+        pos1_t = lists.tile([P, T // 16], U16, name="pos1_t")
+        pos2_t = lists.tile([P, T // 16], U16, name="pos2_t")
+        gate0 = keep.tile([P, T], F32, name="gate0")
+        gate1 = keep.tile([P, T], F32, name="gate1")
+        y = keep.tile([P, SLOTS], F32, name="y")
+        x_codes = [keep.tile([P, T], U32, name=f"x_codes{s}", align_bytes=64) for s in range(PASSES)]
+        x_bytes = [keep.tile([P, T], U8, name=f"x_bytes{s}", align_bytes=64) for s in range(PASSES)]
+        slot_codes = [keep.tile([P, PASSES, PIECE], U32, name=f"slot_codes{i}", align_bytes=64) for i in range(4)]
+        slot_bytes = [keep.tile([P, PASSES, PIECE], U8, name=f"slot_bytes{i}", align_bytes=64) for i in range(4)]
+        warm = keep.tile([P, 1], F32, name="warm")
+
+        nc.gpsimd.memset(warm[:], 0.0)
+        for s in range(PASSES):
+            nc.gpsimd.memset(x_bytes[s][:], 0)
+        nc.scalar.activation(warm[:], warm[:], SIGMOID)
+        nc.sync.dma_start(offs_t[:], offs)
+
+        chunks = []
+        for s in range(PASSES):
+            chunks += [("x", s, 0, 256), ("x", s, 256, 512)]
+        for e in ORDER:
+            chunks += [("w2", e), ("w1", e, 0), ("w1", e, 1), ("w3", e, 0), ("w3", e, 1)]
+        total = len(chunks)
+        last = total - 1
+
+        raw_of = {}
+        grp_of = {}
+        w_codes = {}
+        w_bytes = {}
+
+        def load(i):
+            c = chunks[i]
+            if c[0] == "x":
+                raw = raws.tile([P, J, c[3]], F32, name="raw")
+                src = xT[c[1] * K_PASS : (c[1] + 1) * K_PASS, c[2] : c[2] + c[3]]
+                nc.sync.dma_start(raw[:], src.rearrange("(p j) t -> p j t", j=J))
+                raw_of[i] = [raw]
+            elif c[0] == "w2":
+                raw2 = raws2.tile([P, J, N], F32, name="raw2")
+                nc.sync.dma_start(raw2[:], w2[c[1]].rearrange("(p j) n -> p j n", j=J))
+                raw_of[i] = [raw2]
+            else:
+                w = w1 if c[0] == "w1" else w3
+                rows = w[c[1], c[2] * K_PASS : (c[2] + 1) * K_PASS, :].rearrange("(p j) c -> p j c", j=J)
+                parts = 2 if i == last else 1
+                wide = H // parts
+                tiles = []
+                for part in range(parts):
+                    raw = raws.tile([P, J, wide], F32, name="raw")
+                    nc.sync.dma_start(raw[:], rows[:, :, part * wide : (part + 1) * wide])
+                    tiles.append(raw)
+                raw_of[i] = tiles
+
+        def copy(engine, dst, src):
+            if engine == "V":
+                nc.vector.tensor_copy(dst, src)
+            else:
+                nc.scalar.copy(dst, src)
+
+        state = {"w": 0}
+
+        def interleave(i):
+            c = chunks[i]
+            if c[0] == "x" or c[0] == "w2":
+                wide = c[3] if c[0] == "x" else N
+                if c[0] == "x":
+                    grp = grps.tile([P, wide, J], BF16, name="grp", align_bytes=64)
+                    eng = "V" if wide == 512 else "S"
+                else:
+                    grp = grps.tile([P, wide, J], BF16, name="grp2", align_bytes=64)
+                    eng = "V"
+                copy(eng, grp[:].rearrange("p (c i) j -> p c j i", i=4), raw_of[i][0][:].rearrange("p j (c i) -> p c j i", i=4))
+                grp_of[i] = grp[:].rearrange("p c j -> p (c j)")
+            else:
+                grp = grps.tile([P, J, P, J], BF16, name="grp", align_bytes=64)
+                k = state["w"]
+                state["w"] += 1
+                if i == last:
+                    shares = [(0, 0, 40, "V"), (0, 40, 64, "S"), (1, 64, 104, "V"), (1, 104, 128, "S")]
+                else:
+                    shares = [(0, 0, 128, "V" if k % 4 == 1 else "S")]
+                for part, a, b, eng in shares:
+                    raw = raw_of[i][part]
+                    m0 = part * 64
+                    copy(
+                        eng,
+                        grp[:, :, a:b, :].rearrange("p t m j -> p m j t"),
+                        raw[:, :, 4 * (a - m0) : 4 * (b - m0)].rearrange("p j (m t) -> p m j t", t=4),
+                    )
+                grp_of[i] = grp[:].rearrange("p t m j -> p (t m j)")
+
+        def quantise(i):
+            c = chunks[i]
+            if c[0] == "x":
+                cols = slice(c[2], c[2] + c[3])
+                nc.vector.quantize_mx(x_codes[c[1]][:, cols].bitcast(FP8X4), x_bytes[c[1]][:, cols], grp_of[i])
+                return
+            if c[0] == "w2":
+                w2_c = codes.tile([P, N], U32, name="w2_c", align_bytes=64)
+                w2_b = codes.tile([P, N], U8, name="w2_b", align_bytes=64)
+                nc.vector.quantize_mx(w2_c[:].bitcast(FP8X4), w2_b[:], grp_of[i])
+                w_codes[c] = w2_c
+                w_bytes[c] = w2_b
+                return
+            wc = codes.tile([P, H], U32, name=f"{c[0]}c{c[2]}", align_bytes=64)
+            wb = codes.tile([P, H], U8, name=f"{c[0]}b{c[2]}", align_bytes=64)
+            w_codes[c] = wc
+            w_bytes[c] = wb
+            if i == last:
+                for t in range(4):
+                    nc.vector.quantize_mx(wc[:, t * P : (t + 1) * P].bitcast(FP8X4), wb[:, t * P : (t + 1) * P], grp_of[i][:, t * 512 : (t + 1) * 512])
+            else:
+                nc.vector.quantize_mx(wc[:].bitcast(FP8X4), wb[:], grp_of[i])
+
+        def piece_of(e):
+            return (0, e * UNIT) if e < 3 else (e - 2, 0)
+
+        gathers = []
+        for pc in (1, 0, 2, 3):
+            for s in range(PASSES):
+                gathers += [(pc, s, "codes"), (pc, s, "bytes")]
+
+        def gather(g):
+            pc, s, sort = g
+            cols = offs_t[:, pc * (PIECE // 16) : (pc + 1) * (PIECE // 16)]
+            if sort == "codes":
+                nc.vector.tensor_copy(slot_codes[pc][:, s, :], x_codes[s][:].indirect(cols))
+            else:
+                nc.vector.tensor_copy(slot_bytes[pc][:, s, :], x_bytes[s][:].indirect(cols))
+
+        def product(bank, name, e, u):
+            pc, first = piece_of(e)
+            cols = slice(first + u * UNIT, first + (u + 1) * UNIT)
+            for t in range(4):
+                for s in range(PASSES):
+                    nc.tensor.matmul_mx(
+                        bank[:, t, :],
+                        lhsT=w_codes[(name, e, s)][:, t * P : (t + 1) * P].bitcast(FP8X4),
+                        lhsT_scale=w_bytes[(name, e, s)][:, t * P : (t + 1) * P],
+                        rhs=slot_codes[pc][:, s, cols].bitcast(FP8X4),
+                        rhs_scale=slot_bytes[pc][:, s, cols],
+                        start=(s == 0),
+                        stop=(s == PASSES - 1),
+                    )
+
+        sig_of = {}
+        tasks = {}
+
+        def later(step, task):
+            tasks.setdefault(step, []).append(task)
+
+        def sigmoid(e, u, a):
+            sg = hid.tile([P, UNIT, 4], F32, name="sg")
+            nc.scalar.activation(sg[:], a[:].rearrange("p t n -> p n t"), SIGMOID)
+            sig_of[(e, u)] = sg
+
+        def multiply(e, u, g, hs):
+            h = hid.tile([P, UNIT, 4], BF16, name="h", align_bytes=64)
+            nc.vector.tensor_tensor(h[:], g[:].rearrange("p t n -> p n t"), sig_of[(e, u)][:], MULT)
+            hs[u] = h
+
+        def project(e, u, hs, yb):
+            hc = hid.tile([P, UNIT], U32, name="hc", align_bytes=64)
+            hb = hid.tile([P, UNIT], U8, name="hb", align_bytes=64)
+            nc.vector.quantize_mx(hc[:].bitcast(FP8X4), hb[:], hs[u][:].rearrange("p n t -> p (n t)"))
+            nc.tensor.matmul_mx(
+                yb[:, u * UNIT : (u + 1) * UNIT],
+                lhsT=w_codes[("w2", e)][:].bitcast(FP8X4),
+                lhsT_scale=w_bytes[("w2", e)][:],
+                rhs=hc[:].bitcast(FP8X4),
+                rhs_scale=hb[:],
+                start=True,
+                stop=True,
+            )
+
+        def first_half(e, step):
+            for u in range(COUNTS[e] // UNIT):
+                a = psum_a.tile([P, 4, UNIT], F32, name="a")
+                product(a, "w1", e, u)
+                later(step + 1 + u // 2, lambda u=u, a=a: sigmoid(e, u, a))
+
+        def second_half(e, step):
+            units = COUNTS[e] // UNIT
+            yb = psum_y.tile([P, PIECE], F32, name="yb")
+            hs = {}
+            for u in range(units):
+                g = psum_g.tile([P, 4, UNIT], F32, name="g")
+                product(g, "w3", e, u)
+                later(step + 1 + u // 2, lambda u=u, g=g: multiply(e, u, g, hs))
+                later(step + 2 + u // 2, lambda u=u: project(e, u, hs, yb))
+            later(step + 3 + units // 2, lambda: nc.scalar.copy(y[:, STARTS[e] : STARTS[e] + COUNTS[e]], yb[:, : COUNTS[e]]))
+
+        for i in range(AHEAD):
+            load(i)
+        for i in range(total + 6):
+            if i + AHEAD < total:
+                load(i + AHEAD)
+            if i + AHEAD == total:
+                nc.sync.dma_start(pos1_t[:], pos1)
+                nc.sync.dma_start(pos2_t[:], pos2)
+                nc.sync.dma_start(gate0[:], gate[0])
+                nc.sync.dma_start(gate1[:], gate[1])
+            if i < total:
+                interleave(i)
+            if 0 < i <= total:
+                quantise(i - 1)
+            ready = 2 if i in (5, 6) else 1 if 7 <= i <= 14 or 20 <= i <= 23 else 0
+            for g in gathers[:ready]:
+                gather(g)
+            gathers = gathers[ready:]
+            for task in tasks.get(i, []):
+                task()
+            if 0 < i <= total and chunks[i - 1][0] == "w1" and chunks[i - 1][2] == 1:
+                first_half(chunks[i - 1][1], i)
+            if 0 < i <= total and chunks[i - 1][0] == "w3" and chunks[i - 1][2] == 1:
+                second_half(chunks[i - 1][1], i)
+
+        o1 = keep.tile([P, T], F32, name="o1")
+        nc.vector.tensor_tensor(o1[:], y[:].indirect(pos1_t[:]), gate0[:], MULT)
+        for half in range(2):
+            cols = slice(half * PIECE, (half + 1) * PIECE)
+            o2 = keep.tile([P, PIECE], F32, name=f"o2_{half}")
+            total_out = keep.tile([P, PIECE], F32, name=f"total_out{half}")
+            nc.vector.tensor_tensor(o2[:], y[:].indirect(pos2_t[:, half * 24 : (half + 1) * 24]), gate1[:, cols], MULT)
+            nc.vector.tensor_tensor(total_out[:], o1[:, cols], o2[:], ADD)
+            nc.sync.dma_start(out[:, cols], total_out[:])

@@ -1,12 +1,13 @@
 from contextlib import ExitStack
 
 import concourse.mybir as mybir
+from concourse.masks import make_identity
 
 T, E, H, N = 768, 6, 512, 128
 SLOTS = 1536
 STARTS = (0, 128, 256, 384, 768, 1152)
 COUNTS = (128, 128, 128, 384, 384, 384)
-ORDER = (3, 0, 4, 1, 5, 2)
+ORDER = (3, 4, 5, 0, 1, 2)
 FLOPS = 3422552064
 
 P = 128
@@ -15,7 +16,9 @@ K_PASS = 512
 PASSES = 2
 PIECE = 384
 UNIT = 128
-AHEAD = 9
+V_CHUNKS = (1,)
+RAW_BUFS = 8
+GRP_BUFS = 6
 
 F32 = mybir.dt.float32
 BF16 = mybir.dt.bfloat16
@@ -33,41 +36,48 @@ def tile_moe_rag_glu_sigmoid_kernel(tc, xT, w1, w3, w2, gate, offs, pos1, pos2, 
     with ExitStack() as ctx:
         lists = ctx.enter_context(tc.tile_pool(name="lists", bufs=1))
         keep = ctx.enter_context(tc.tile_pool(name="keep", bufs=1))
-        raws = ctx.enter_context(tc.tile_pool(name="raws", bufs=11))
+        raws = ctx.enter_context(tc.tile_pool(name="raws", bufs=RAW_BUFS))
         raws2 = ctx.enter_context(tc.tile_pool(name="raws2", bufs=3))
-        grps = ctx.enter_context(tc.tile_pool(name="grps", bufs=4))
+        grps = ctx.enter_context(tc.tile_pool(name="grps", bufs=GRP_BUFS))
         codes = ctx.enter_context(tc.tile_pool(name="codes", bufs=3))
+        slots = ctx.enter_context(tc.tile_pool(name="slots", bufs=2))
         hid = ctx.enter_context(tc.tile_pool(name="hid", bufs=6))
-        psum_a = ctx.enter_context(tc.psum_pool(name="psum_a", bufs=3))
-        psum_g = ctx.enter_context(tc.psum_pool(name="psum_g", bufs=3))
+        psum_a = ctx.enter_context(tc.psum_pool(name="psum_a", bufs=2))
+        psum_g = ctx.enter_context(tc.psum_pool(name="psum_g", bufs=2))
+        psum_t = ctx.enter_context(tc.psum_pool(name="psum_t", bufs=2))
         psum_y = ctx.enter_context(tc.psum_pool(name="psum_y", bufs=2))
 
         offs_t = lists.tile([P, SLOTS // 16], U16, name="offs_t")
         pos1_t = lists.tile([P, T // 16], U16, name="pos1_t")
         pos2_t = lists.tile([P, T // 16], U16, name="pos2_t")
-        gate0 = keep.tile([P, T], F32, name="gate0")
-        gate1 = keep.tile([P, T], F32, name="gate1")
         y = keep.tile([P, SLOTS], F32, name="y")
         x_codes = [keep.tile([P, T], U32, name=f"x_codes{s}", align_bytes=64) for s in range(PASSES)]
         x_bytes = [keep.tile([P, T], U8, name=f"x_bytes{s}", align_bytes=64) for s in range(PASSES)]
-        slot_codes = [keep.tile([P, PASSES, PIECE], U32, name=f"slot_codes{i}", align_bytes=64) for i in range(4)]
-        slot_bytes = [keep.tile([P, PASSES, PIECE], U8, name=f"slot_bytes{i}", align_bytes=64) for i in range(4)]
+        ident = keep.tile([P, P], F32, name="ident")
         warm = keep.tile([P, 1], F32, name="warm")
 
         nc.gpsimd.memset(warm[:], 0.0)
         for s in range(PASSES):
             nc.gpsimd.memset(x_bytes[s][:], 0)
+        make_identity(nc, ident[:])
         nc.scalar.activation(warm[:], warm[:], SIGMOID)
         nc.sync.dma_start(offs_t[:], offs)
 
         chunks = []
         for s in range(PASSES):
-            chunks += [("x", s, 0, 256), ("x", s, 256, 512)]
+            chunks += [("x", s, 0, 256), ("x", s, 256, 768)]
         for e in ORDER:
-            chunks += [("w2", e), ("w1", e, 0), ("w1", e, 1), ("w3", e, 0), ("w3", e, 1)]
+            chunks += [("w2", e)]
+            for name in ("w1", "w3"):
+                for s in range(PASSES):
+                    if (name, e, s) == ("w3", ORDER[-1], 1):
+                        chunks += [(name, e, s, 0, 256), (name, e, s, 256, 512)]
+                    else:
+                        chunks += [(name, e, s, 0, 512)]
         total = len(chunks)
-        last = total - 1
+        chunks += [("gate", 0), ("gate", 1)]
 
+        gates = []
         raw_of = {}
         grp_of = {}
         w_codes = {}
@@ -75,141 +85,141 @@ def tile_moe_rag_glu_sigmoid_kernel(tc, xT, w1, w3, w2, gate, offs, pos1, pos2, 
 
         def load(i):
             c = chunks[i]
-            if c[0] == "x":
-                raw = raws.tile([P, J, c[3]], F32, name="raw")
-                src = xT[c[1] * K_PASS : (c[1] + 1) * K_PASS, c[2] : c[2] + c[3]]
-                nc.sync.dma_start(raw[:], src.rearrange("(p j) t -> p j t", j=J))
-                raw_of[i] = [raw]
+            if c[0] == "gate":
+                raw = raws.tile([P, T], F32, name="raw")
+                nc.sync.dma_start(raw[:], gate[c[1]])
+                gates.append(raw)
             elif c[0] == "w2":
                 raw2 = raws2.tile([P, J, N], F32, name="raw2")
                 nc.sync.dma_start(raw2[:], w2[c[1]].rearrange("(p j) n -> p j n", j=J))
-                raw_of[i] = [raw2]
+                raw_of[i] = raw2
             else:
-                w = w1 if c[0] == "w1" else w3
-                rows = w[c[1], c[2] * K_PASS : (c[2] + 1) * K_PASS, :].rearrange("(p j) c -> p j c", j=J)
-                parts = 2 if i == last else 1
-                wide = H // parts
-                tiles = []
-                for part in range(parts):
-                    raw = raws.tile([P, J, wide], F32, name="raw")
-                    nc.sync.dma_start(raw[:], rows[:, :, part * wide : (part + 1) * wide])
-                    tiles.append(raw)
-                raw_of[i] = tiles
-
-        def copy(engine, dst, src):
-            if engine == "V":
-                nc.vector.tensor_copy(dst, src)
-            else:
-                nc.scalar.copy(dst, src)
-
-        state = {"w": 0}
+                if c[0] == "x":
+                    k0, c0, c1 = c[1] * K_PASS, c[2], c[3]
+                    src = xT[k0 : k0 + K_PASS, c0:c1]
+                else:
+                    k0, c0, c1 = c[2] * K_PASS, c[3], c[4]
+                    w = w1 if c[0] == "w1" else w3
+                    src = w[c[1], k0 : k0 + K_PASS, c0:c1]
+                raw = raws.tile([P, J, c1 - c0], F32, name="raw")
+                nc.sync.dma_start(raw[:], src.rearrange("(p j) c -> p j c", j=J))
+                raw_of[i] = raw
 
         def interleave(i):
             c = chunks[i]
-            if c[0] == "x" or c[0] == "w2":
-                wide = c[3] if c[0] == "x" else N
-                if c[0] == "x":
-                    grp = grps.tile([P, wide, J], BF16, name="grp", align_bytes=64)
-                    eng = "V" if wide == 512 else "S"
-                else:
-                    grp = grps.tile([P, wide, J], BF16, name="grp2", align_bytes=64)
-                    eng = "V"
-                copy(eng, grp[:].rearrange("p (c i) j -> p c j i", i=4), raw_of[i][0][:].rearrange("p j (c i) -> p c j i", i=4))
-                grp_of[i] = grp[:].rearrange("p c j -> p (c j)")
+            raw = raw_of[i]
+            if c[0] == "w2":
+                wide = N
+                grp = grps.tile([P, wide, J], BF16, name="grp2", align_bytes=64)
+                shares = [(0, wide, "V")]
             else:
-                grp = grps.tile([P, J, P, J], BF16, name="grp", align_bytes=64)
-                k = state["w"]
-                state["w"] += 1
-                if i == last:
-                    shares = [(0, 0, 40, "V"), (0, 40, 64, "S"), (1, 64, 104, "V"), (1, 104, 128, "S")]
+                wide = c[-1] - c[-2]
+                grp = grps.tile([P, wide, J], BF16, name="grp", align_bytes=64)
+                if c[0] == "x":
+                    shares = [(0, wide, "V" if wide == 512 else "S")]
+                elif wide == 256:
+                    shares = [(0, 160, "V"), (160, 256, "S")]
                 else:
-                    shares = [(0, 0, 128, "V" if k % 4 == 1 else "S")]
-                for part, a, b, eng in shares:
-                    raw = raw_of[i][part]
-                    m0 = part * 64
-                    copy(
-                        eng,
-                        grp[:, :, a:b, :].rearrange("p t m j -> p m j t"),
-                        raw[:, :, 4 * (a - m0) : 4 * (b - m0)].rearrange("p j (m t) -> p m j t", t=4),
-                    )
-                grp_of[i] = grp[:].rearrange("p t m j -> p (t m j)")
+                    k = ("w1", "w3").index(c[0]) * 2 + c[2]
+                    shares = [(0, wide, "V" if k in V_CHUNKS else "S")]
+            for a, b, eng in shares:
+                dst = grp[:, a:b, :].rearrange("p (c i) j -> p c j i", i=4)
+                src = raw[:, :, a:b].rearrange("p j (c i) -> p c j i", i=4)
+                if eng == "V":
+                    nc.vector.tensor_copy(dst, src)
+                else:
+                    nc.scalar.copy(dst, src)
+            grp_of[i] = grp[:].rearrange("p c j -> p (c j)")
 
         def quantise(i):
             c = chunks[i]
             if c[0] == "x":
-                cols = slice(c[2], c[2] + c[3])
-                nc.vector.quantize_mx(x_codes[c[1]][:, cols].bitcast(FP8X4), x_bytes[c[1]][:, cols], grp_of[i])
-                return
-            if c[0] == "w2":
-                w2_c = codes.tile([P, N], U32, name="w2_c", align_bytes=64)
-                w2_b = codes.tile([P, N], U8, name="w2_b", align_bytes=64)
-                nc.vector.quantize_mx(w2_c[:].bitcast(FP8X4), w2_b[:], grp_of[i])
-                w_codes[c] = w2_c
-                w_bytes[c] = w2_b
-                return
-            wc = codes.tile([P, H], U32, name=f"{c[0]}c{c[2]}", align_bytes=64)
-            wb = codes.tile([P, H], U8, name=f"{c[0]}b{c[2]}", align_bytes=64)
-            w_codes[c] = wc
-            w_bytes[c] = wb
-            if i == last:
-                for t in range(4):
-                    nc.vector.quantize_mx(wc[:, t * P : (t + 1) * P].bitcast(FP8X4), wb[:, t * P : (t + 1) * P], grp_of[i][:, t * 512 : (t + 1) * 512])
+                cc, cb, cols = x_codes[c[1]], x_bytes[c[1]], slice(c[2], c[3])
+            elif c[0] == "w2":
+                cc = codes.tile([P, N], U32, name="w2_c", align_bytes=64)
+                cb = codes.tile([P, N], U8, name="w2_b", align_bytes=64)
+                w_codes[c], w_bytes[c] = cc, cb
+                cols = slice(0, N)
             else:
-                nc.vector.quantize_mx(wc[:].bitcast(FP8X4), wb[:], grp_of[i])
+                if c[3] == 0:
+                    cc = codes.tile([P, H], U32, name=f"{c[0]}c{c[2]}", align_bytes=64)
+                    cb = codes.tile([P, H], U8, name=f"{c[0]}b{c[2]}", align_bytes=64)
+                    w_codes[c[:3]], w_bytes[c[:3]] = cc, cb
+                cc, cb, cols = w_codes[c[:3]], w_bytes[c[:3]], slice(c[3], c[4])
+            nc.vector.quantize_mx(cc[:, cols].bitcast(FP8X4), cb[:, cols], grp_of[i])
 
         def piece_of(e):
             return (0, e * UNIT) if e < 3 else (e - 2, 0)
 
-        gathers = []
-        for pc in (1, 0, 2, 3):
-            for s in range(PASSES):
-                gathers += [(pc, s, "codes"), (pc, s, "bytes")]
+        slot_codes = {}
+        slot_bytes = {}
 
-        def gather(g):
-            pc, s, sort = g
+        def gather(pc, s, sort):
+            if pc not in slot_codes:
+                slot_codes[pc] = slots.tile([P, PASSES, PIECE], U32, name="sc", align_bytes=64)
+                slot_bytes[pc] = slots.tile([P, PASSES, PIECE], U8, name="sb", align_bytes=64)
             cols = offs_t[:, pc * (PIECE // 16) : (pc + 1) * (PIECE // 16)]
             if sort == "codes":
                 nc.vector.tensor_copy(slot_codes[pc][:, s, :], x_codes[s][:].indirect(cols))
             else:
                 nc.vector.tensor_copy(slot_bytes[pc][:, s, :], x_bytes[s][:].indirect(cols))
 
-        def product(bank, name, e, u):
+        def product(bank, name, e, u, c0, c1):
             pc, first = piece_of(e)
-            cols = slice(first + u * UNIT, first + (u + 1) * UNIT)
-            for t in range(4):
-                for s in range(PASSES):
-                    nc.tensor.matmul_mx(
-                        bank[:, t, :],
-                        lhsT=w_codes[(name, e, s)][:, t * P : (t + 1) * P].bitcast(FP8X4),
-                        lhsT_scale=w_bytes[(name, e, s)][:, t * P : (t + 1) * P],
-                        rhs=slot_codes[pc][:, s, cols].bitcast(FP8X4),
-                        rhs_scale=slot_bytes[pc][:, s, cols],
-                        start=(s == 0),
-                        stop=(s == PASSES - 1),
-                    )
+            mine = slice(first + u * UNIT, first + (u + 1) * UNIT)
+            for s in range(PASSES):
+                nc.tensor.matmul_mx(
+                    bank[:, c0:c1],
+                    lhsT=slot_codes[pc][:, s, mine].bitcast(FP8X4),
+                    lhsT_scale=slot_bytes[pc][:, s, mine],
+                    rhs=w_codes[(name, e, s)][:, c0:c1].bitcast(FP8X4),
+                    rhs_scale=w_bytes[(name, e, s)][:, c0:c1],
+                    start=(s == 0),
+                    stop=(s == PASSES - 1),
+                )
 
-        sig_of = {}
         tasks = {}
 
         def later(step, task):
             tasks.setdefault(step, []).append(task)
 
-        def sigmoid(e, u, a):
-            sg = hid.tile([P, UNIT, 4], F32, name="sg")
-            nc.scalar.activation(sg[:], a[:].rearrange("p t n -> p n t"), SIGMOID)
-            sig_of[(e, u)] = sg
+        state = {}
 
-        def multiply(e, u, g, hs):
-            h = hid.tile([P, UNIT, 4], BF16, name="h", align_bytes=64)
-            nc.vector.tensor_tensor(h[:], g[:].rearrange("p t n -> p n t"), sig_of[(e, u)][:], MULT)
-            hs[u] = h
+        def gate_half(e, u):
+            a = psum_a.tile([P, H], F32, name="a")
+            product(a, "w1", e, u, 0, H)
+            sg = hid.tile([P, H], F32, name="sg")
+            nc.scalar.activation(sg[:], a[:], SIGMOID)
+            state[("sg", e, u)] = sg
 
-        def project(e, u, hs, yb):
+        def value_half(e, u, parts):
+            g = psum_g.tile([P, H], F32, name="g")
+            h = hid.tile([P, H], BF16, name="h", align_bytes=64)
+            wide = H // parts
+            for k in range(parts):
+                c0, c1 = k * wide, (k + 1) * wide
+                product(g, "w3", e, u, c0, c1)
+                nc.vector.tensor_tensor(h[:, c0:c1], g[:, c0:c1], state[("sg", e, u)][:, c0:c1], MULT)
+            state[("h", e, u)] = h
+
+        def turn(e, u):
+            words = state[("h", e, u)][:].bitcast(F32)
+            tr = psum_t.tile([P, 2, UNIT], F32, name="tr")
+            for k in range(2):
+                nc.tensor.transpose(tr[:, k, :], words[:, k : 2 * UNIT : 2], ident[:])
+            ht = hid.tile([P, UNIT, J], BF16, name="ht", align_bytes=64)
+            nc.scalar.copy(ht[:].bitcast(F32), tr[:].rearrange("p k r -> p r k"))
+            state[("ht", e, u)] = ht
+
+        def project(e, u):
             hc = hid.tile([P, UNIT], U32, name="hc", align_bytes=64)
             hb = hid.tile([P, UNIT], U8, name="hb", align_bytes=64)
-            nc.vector.quantize_mx(hc[:].bitcast(FP8X4), hb[:], hs[u][:].rearrange("p n t -> p (n t)"))
+            nc.vector.quantize_mx(hc[:].bitcast(FP8X4), hb[:], state[("ht", e, u)][:].rearrange("p r j -> p (r j)"))
+            if u == 0:
+                yb = psum_y.tile([P, PIECE], F32, name="yb")
+                state[("y", e)] = yb
             nc.tensor.matmul_mx(
-                yb[:, u * UNIT : (u + 1) * UNIT],
+                state[("y", e)][:, u * UNIT : (u + 1) * UNIT],
                 lhsT=w_codes[("w2", e)][:].bitcast(FP8X4),
                 lhsT_scale=w_bytes[("w2", e)][:],
                 rhs=hc[:].bitcast(FP8X4),
@@ -218,54 +228,51 @@ def tile_moe_rag_glu_sigmoid_kernel(tc, xT, w1, w3, w2, gate, offs, pos1, pos2, 
                 stop=True,
             )
 
-        def first_half(e, step):
-            for u in range(COUNTS[e] // UNIT):
-                a = psum_a.tile([P, 4, UNIT], F32, name="a")
-                product(a, "w1", e, u)
-                later(step + 1 + u // 2, lambda u=u, a=a: sigmoid(e, u, a))
+        def leave(e):
+            nc.scalar.copy(y[:, STARTS[e] : STARTS[e] + COUNTS[e]], state[("y", e)][:, : COUNTS[e]])
 
-        def second_half(e, step):
-            units = COUNTS[e] // UNIT
-            yb = psum_y.tile([P, PIECE], F32, name="yb")
-            hs = {}
-            for u in range(units):
-                g = psum_g.tile([P, 4, UNIT], F32, name="g")
-                product(g, "w3", e, u)
-                later(step + 1 + u // 2, lambda u=u, g=g: multiply(e, u, g, hs))
-                later(step + 2 + u // 2, lambda u=u: project(e, u, hs, yb))
-            later(step + 3 + units // 2, lambda: nc.scalar.copy(y[:, STARTS[e] : STARTS[e] + COUNTS[e]], yb[:, : COUNTS[e]]))
+        gather_steps = {}
+        for first, pc in ((5, 1), (8, 2), (12, 3), (18, 0)):
+            for s in range(PASSES):
+                for k, sort in enumerate(("codes", "bytes")):
+                    gather_steps.setdefault(first + (s if first == 5 else 2 * s + k), []).append((pc, s, sort))
 
-        for i in range(AHEAD):
+        for i in range(RAW_BUFS):
             load(i)
         for i in range(total + 6):
-            if i + AHEAD < total:
-                load(i + AHEAD)
-            if i + AHEAD == total:
-                nc.sync.dma_start(pos1_t[:], pos1)
-                nc.sync.dma_start(pos2_t[:], pos2)
-                nc.sync.dma_start(gate0[:], gate[0])
-                nc.sync.dma_start(gate1[:], gate[1])
             if i < total:
                 interleave(i)
+            if i + RAW_BUFS < len(chunks):
+                load(i + RAW_BUFS)
+            if i == RAW_BUFS:
+                nc.sync.dma_start(pos1_t[:], pos1)
+                nc.sync.dma_start(pos2_t[:], pos2)
             if 0 < i <= total:
                 quantise(i - 1)
-            ready = 2 if i in (5, 6) else 1 if 7 <= i <= 14 or 20 <= i <= 23 else 0
-            for g in gathers[:ready]:
-                gather(g)
-            gathers = gathers[ready:]
+            for g in gather_steps.get(i, []):
+                gather(*g)
+            done = chunks[i - 1] if 0 < i <= total else ("none",)
+            if done[0] in ("w1", "w3") and done[2] == 1 and done[4] == H:
+                e = done[1]
+                lag = 0 if e == ORDER[-1] else 1
+                for u in range(COUNTS[e] // UNIT):
+                    if done[0] == "w1":
+                        later(i + lag * u, lambda e=e, u=u: gate_half(e, u))
+                    else:
+                        later(i + lag * u, lambda e=e, u=u, parts=1 if lag else 2: value_half(e, u, parts))
+                        later(i + lag * (u + 1), lambda e=e, u=u: turn(e, u))
+                        later(i + lag * (u + 2), lambda e=e, u=u: project(e, u))
+                if done[0] == "w3":
+                    later(i + lag * (COUNTS[e] // UNIT + 2), lambda e=e: leave(e))
             for task in tasks.get(i, []):
                 task()
-            if 0 < i <= total and chunks[i - 1][0] == "w1" and chunks[i - 1][2] == 1:
-                first_half(chunks[i - 1][1], i)
-            if 0 < i <= total and chunks[i - 1][0] == "w3" and chunks[i - 1][2] == 1:
-                second_half(chunks[i - 1][1], i)
 
         o1 = keep.tile([P, T], F32, name="o1")
-        nc.vector.tensor_tensor(o1[:], y[:].indirect(pos1_t[:]), gate0[:], MULT)
+        nc.vector.tensor_tensor(o1[:], y[:].indirect(pos1_t[:]), gates[0][:], MULT)
         for half in range(2):
             cols = slice(half * PIECE, (half + 1) * PIECE)
             o2 = keep.tile([P, PIECE], F32, name=f"o2_{half}")
             total_out = keep.tile([P, PIECE], F32, name=f"total_out{half}")
-            nc.vector.tensor_tensor(o2[:], y[:].indirect(pos2_t[:, half * 24 : (half + 1) * 24]), gate1[:, cols], MULT)
+            nc.vector.tensor_tensor(o2[:], y[:].indirect(pos2_t[:, half * 24 : (half + 1) * 24]), gates[1][:, cols], MULT)
             nc.vector.tensor_tensor(total_out[:], o1[:, cols], o2[:], ADD)
             nc.sync.dma_start(out[:, cols], total_out[:])

@@ -16,9 +16,10 @@ K_PASS = 512
 PASSES = 2
 PIECE = 384
 UNIT = 128
-V_CHUNKS = (1,)
-RAW_BUFS = 8
-GRP_BUFS = 6
+V_CHUNKS = {3: (2, 3), 4: (2, 3), 5: (2, 3), 0: (2, 3), 1: (2, 3), 2: (1, 2)}
+RING = 9
+GRP_BUFS = 8
+GATHER_STEPS = ((5, 1), (7, 2), (10, 3), (13, 0))
 
 F32 = mybir.dt.float32
 BF16 = mybir.dt.bfloat16
@@ -36,29 +37,27 @@ def tile_moe_rag_glu_sigmoid_kernel(tc, xT, w1, w3, w2, gate, offs, pos1, pos2, 
     with ExitStack() as ctx:
         lists = ctx.enter_context(tc.tile_pool(name="lists", bufs=1))
         keep = ctx.enter_context(tc.tile_pool(name="keep", bufs=1))
-        raws = ctx.enter_context(tc.tile_pool(name="raws", bufs=RAW_BUFS))
+        raws = ctx.enter_context(tc.tile_pool(name="raws", bufs=1))
         raws2 = ctx.enter_context(tc.tile_pool(name="raws2", bufs=3))
         grps = ctx.enter_context(tc.tile_pool(name="grps", bufs=GRP_BUFS))
         codes = ctx.enter_context(tc.tile_pool(name="codes", bufs=3))
         slots = ctx.enter_context(tc.tile_pool(name="slots", bufs=2))
         hid = ctx.enter_context(tc.tile_pool(name="hid", bufs=6))
-        psum_a = ctx.enter_context(tc.psum_pool(name="psum_a", bufs=2))
-        psum_g = ctx.enter_context(tc.psum_pool(name="psum_g", bufs=2))
+        psum_a = ctx.enter_context(tc.psum_pool(name="psum_a", bufs=1))
+        psum_g = ctx.enter_context(tc.psum_pool(name="psum_g", bufs=1))
         psum_t = ctx.enter_context(tc.psum_pool(name="psum_t", bufs=2))
-        psum_y = ctx.enter_context(tc.psum_pool(name="psum_y", bufs=2))
 
         offs_t = lists.tile([P, SLOTS // 16], U16, name="offs_t")
         pos1_t = lists.tile([P, T // 16], U16, name="pos1_t")
         pos2_t = lists.tile([P, T // 16], U16, name="pos2_t")
         y = keep.tile([P, SLOTS], F32, name="y")
         x_codes = [keep.tile([P, T], U32, name=f"x_codes{s}", align_bytes=64) for s in range(PASSES)]
-        x_bytes = [keep.tile([P, T], U8, name=f"x_bytes{s}", align_bytes=64) for s in range(PASSES)]
+        x_bytes = keep.tile([P, T], U8, name="x_bytes", align_bytes=64)
         ident = keep.tile([P, P], F32, name="ident")
         warm = keep.tile([P, 1], F32, name="warm")
 
         nc.gpsimd.memset(warm[:], 0.0)
-        for s in range(PASSES):
-            nc.gpsimd.memset(x_bytes[s][:], 0)
+        nc.gpsimd.memset(x_bytes[:], 0)
         make_identity(nc, ident[:])
         nc.scalar.activation(warm[:], warm[:], SIGMOID)
         nc.sync.dma_start(offs_t[:], offs)
@@ -83,10 +82,24 @@ def tile_moe_rag_glu_sigmoid_kernel(tc, xT, w1, w3, w2, gate, offs, pos1, pos2, 
         w_codes = {}
         w_bytes = {}
 
+        ring = []
+
+        def ring_tile(shape, dtype):
+            n = len(ring)
+            assert n < RING or ring[n - RING]["free"]
+            tile = raws.tile(shape, dtype, name=f"ring{n % RING}", align_bytes=64)
+            ring.append({"free": False})
+            return tile, ring[-1]
+
+        def room():
+            return len(ring) < RING or ring[len(ring) - RING]["free"]
+
+        entry_of = {}
+
         def load(i):
             c = chunks[i]
             if c[0] == "gate":
-                raw = raws.tile([P, T], F32, name="raw")
+                raw, entry_of[i] = ring_tile([P, T], F32)
                 nc.sync.dma_start(raw[:], gate[c[1]])
                 gates.append(raw)
             elif c[0] == "w2":
@@ -101,7 +114,7 @@ def tile_moe_rag_glu_sigmoid_kernel(tc, xT, w1, w3, w2, gate, offs, pos1, pos2, 
                     k0, c0, c1 = c[2] * K_PASS, c[3], c[4]
                     w = w1 if c[0] == "w1" else w3
                     src = w[c[1], k0 : k0 + K_PASS, c0:c1]
-                raw = raws.tile([P, J, c1 - c0], F32, name="raw")
+                raw, entry_of[i] = ring_tile([P, J, c1 - c0], F32)
                 nc.sync.dma_start(raw[:], src.rearrange("(p j) c -> p j c", j=J))
                 raw_of[i] = raw
 
@@ -121,7 +134,7 @@ def tile_moe_rag_glu_sigmoid_kernel(tc, xT, w1, w3, w2, gate, offs, pos1, pos2, 
                     shares = [(0, 160, "V"), (160, 256, "S")]
                 else:
                     k = ("w1", "w3").index(c[0]) * 2 + c[2]
-                    shares = [(0, wide, "V" if k in V_CHUNKS else "S")]
+                    shares = [(0, wide, "V" if k in V_CHUNKS[c[1]] else "S")]
             for a, b, eng in shares:
                 dst = grp[:, a:b, :].rearrange("p (c i) j -> p c j i", i=4)
                 src = raw[:, :, a:b].rearrange("p j (c i) -> p c j i", i=4)
@@ -130,12 +143,16 @@ def tile_moe_rag_glu_sigmoid_kernel(tc, xT, w1, w3, w2, gate, offs, pos1, pos2, 
                 else:
                     nc.scalar.copy(dst, src)
             grp_of[i] = grp[:].rearrange("p c j -> p (c j)")
+            if c[0] != "w2":
+                entry_of[i]["free"] = True
 
         def quantise(i):
             c = chunks[i]
             if c[0] == "x":
-                cc, cb, cols = x_codes[c[1]], x_bytes[c[1]], slice(c[2], c[3])
-            elif c[0] == "w2":
+                cols = slice(c[2], c[3])
+                nc.vector.quantize_mx(x_codes[c[1]][:, cols].bitcast(FP8X4), x_bytes[4 * c[1] : P, cols], grp_of[i])
+                return
+            if c[0] == "w2":
                 cc = codes.tile([P, N], U32, name="w2_c", align_bytes=64)
                 cb = codes.tile([P, N], U8, name="w2_b", align_bytes=64)
                 w_codes[c], w_bytes[c] = cc, cb
@@ -157,12 +174,12 @@ def tile_moe_rag_glu_sigmoid_kernel(tc, xT, w1, w3, w2, gate, offs, pos1, pos2, 
         def gather(pc, s, sort):
             if pc not in slot_codes:
                 slot_codes[pc] = slots.tile([P, PASSES, PIECE], U32, name="sc", align_bytes=64)
-                slot_bytes[pc] = slots.tile([P, PASSES, PIECE], U8, name="sb", align_bytes=64)
+                slot_bytes[pc] = slots.tile([P, PIECE], U8, name="sb", align_bytes=64)
             cols = offs_t[:, pc * (PIECE // 16) : (pc + 1) * (PIECE // 16)]
             if sort == "codes":
                 nc.vector.tensor_copy(slot_codes[pc][:, s, :], x_codes[s][:].indirect(cols))
             else:
-                nc.vector.tensor_copy(slot_bytes[pc][:, s, :], x_bytes[s][:].indirect(cols))
+                nc.vector.tensor_copy(slot_bytes[pc][:], x_bytes[:].indirect(cols))
 
         def product(bank, name, e, u, c0, c1):
             pc, first = piece_of(e)
@@ -171,7 +188,7 @@ def tile_moe_rag_glu_sigmoid_kernel(tc, xT, w1, w3, w2, gate, offs, pos1, pos2, 
                 nc.tensor.matmul_mx(
                     bank[:, c0:c1],
                     lhsT=slot_codes[pc][:, s, mine].bitcast(FP8X4),
-                    lhsT_scale=slot_bytes[pc][:, s, mine],
+                    lhsT_scale=slot_bytes[pc][4 * s : P, mine],
                     rhs=w_codes[(name, e, s)][:, c0:c1].bitcast(FP8X4),
                     rhs_scale=w_bytes[(name, e, s)][:, c0:c1],
                     start=(s == 0),
@@ -185,87 +202,119 @@ def tile_moe_rag_glu_sigmoid_kernel(tc, xT, w1, w3, w2, gate, offs, pos1, pos2, 
 
         state = {}
 
-        def gate_half(e, u):
-            a = psum_a.tile([P, H], F32, name="a")
-            product(a, "w1", e, u, 0, H)
-            sg = hid.tile([P, H], F32, name="sg")
-            nc.scalar.activation(sg[:], a[:], SIGMOID)
-            state[("sg", e, u)] = sg
+        def units(e):
+            return range(COUNTS[e] // UNIT)
 
-        def value_half(e, u, parts):
-            g = psum_g.tile([P, H], F32, name="g")
-            h = hid.tile([P, H], BF16, name="h", align_bytes=64)
+        def first_products(e):
+            for u in units(e):
+                name = "ay" if u == units(e)[-1] else f"a{u}"
+                a = psum_a.tile([P, H], F32, name=name)
+                product(a, "w1", e, u, 0, H)
+                state[("a", e, u)] = a
+
+        def sigmoids(e):
+            sg, state[("sg_entry", e)] = ring_tile([P, len(units(e)), H], F32)
+            for u in units(e):
+                nc.scalar.activation(sg[:, u, :], state[("a", e, u)][:], SIGMOID)
+            state[("sg", e)] = sg
+
+        def second_products(e, parts):
             wide = H // parts
-            for k in range(parts):
-                c0, c1 = k * wide, (k + 1) * wide
-                product(g, "w3", e, u, c0, c1)
-                nc.vector.tensor_tensor(h[:, c0:c1], g[:, c0:c1], state[("sg", e, u)][:, c0:c1], MULT)
-            state[("h", e, u)] = h
+            for u in units(e):
+                g = psum_g.tile([P, H], F32, name=f"g{u}")
+                for k in range(parts):
+                    product(g, "w3", e, u, k * wide, (k + 1) * wide)
+                state[("g", e, u)] = g
 
-        def turn(e, u):
-            words = state[("h", e, u)][:].bitcast(F32)
-            tr = psum_t.tile([P, 2, UNIT], F32, name="tr")
-            for k in range(2):
-                nc.tensor.transpose(tr[:, k, :], words[:, k : 2 * UNIT : 2], ident[:])
-            ht = hid.tile([P, UNIT, J], BF16, name="ht", align_bytes=64)
-            nc.scalar.copy(ht[:].bitcast(F32), tr[:].rearrange("p k r -> p r k"))
-            state[("ht", e, u)] = ht
+        def multiply(e, parts):
+            wide = H // parts
+            for u in units(e):
+                h = hid.tile([P, H], BF16, name="h", align_bytes=64)
+                for k in range(parts):
+                    cols = slice(k * wide, (k + 1) * wide)
+                    nc.vector.tensor_tensor(h[:, cols], state[("g", e, u)][:, cols], state[("sg", e)][:, u, cols], MULT)
+                words = h[:].bitcast(F32)
+                if u % 2 == 0:
+                    tr = psum_t.tile([P, 4, UNIT], F32, name="tr")
+                half = tr[:, 2 * (u % 2) : 2 * (u % 2) + 2, :]
+                for k in range(2):
+                    nc.tensor.transpose(half[:, k, :], words[:, k : 2 * UNIT : 2], ident[:])
+                state[("tr", e, u)] = half
+            state[("sg_entry", e)]["free"] = True
 
-        def project(e, u):
-            hc = hid.tile([P, UNIT], U32, name="hc", align_bytes=64)
-            hb = hid.tile([P, UNIT], U8, name="hb", align_bytes=64)
-            nc.vector.quantize_mx(hc[:].bitcast(FP8X4), hb[:], state[("ht", e, u)][:].rearrange("p r j -> p (r j)"))
-            if u == 0:
-                yb = psum_y.tile([P, PIECE], F32, name="yb")
-                state[("y", e)] = yb
-            nc.tensor.matmul_mx(
-                state[("y", e)][:, u * UNIT : (u + 1) * UNIT],
-                lhsT=w_codes[("w2", e)][:].bitcast(FP8X4),
-                lhsT_scale=w_bytes[("w2", e)][:],
-                rhs=hc[:].bitcast(FP8X4),
-                rhs_scale=hb[:],
-                start=True,
-                stop=True,
-            )
+        def turn(e):
+            if e == ORDER[-1]:
+                ht = hid.tile([P, 3, UNIT, J], BF16, name="ht", align_bytes=64)
+                entry = {}
+            else:
+                ht, entry = ring_tile([P, len(units(e)), UNIT, J], BF16)
+            for u in units(e):
+                nc.scalar.copy(ht[:, u, :, :].bitcast(F32), state[("tr", e, u)].rearrange("p k r -> p r k"))
+            for u in units(e):
+                hc = hid.tile([P, UNIT], U32, name="hc", align_bytes=64)
+                hb = hid.tile([P, UNIT], U8, name="hb", align_bytes=64)
+                nc.vector.quantize_mx(hc[:].bitcast(FP8X4), hb[:], ht[:, u, :, :].rearrange("p r j -> p (r j)"))
+                state[("hc", e, u)] = (hc, hb)
+            entry["free"] = True
 
-        def leave(e):
-            nc.scalar.copy(y[:, STARTS[e] : STARTS[e] + COUNTS[e]], state[("y", e)][:, : COUNTS[e]])
+        def project(e):
+            yb = psum_a.tile([P, PIECE], F32, name="ay")
+            for u in units(e):
+                hc, hb = state[("hc", e, u)]
+                nc.tensor.matmul_mx(
+                    yb[:, u * UNIT : (u + 1) * UNIT],
+                    lhsT=w_codes[("w2", e)][:].bitcast(FP8X4),
+                    lhsT_scale=w_bytes[("w2", e)][:],
+                    rhs=hc[:].bitcast(FP8X4),
+                    rhs_scale=hb[:],
+                    start=True,
+                    stop=True,
+                )
+            nc.scalar.copy(y[:, STARTS[e] : STARTS[e] + COUNTS[e]], yb[:, : COUNTS[e]])
 
         gather_steps = {}
-        for first, pc in ((5, 1), (8, 2), (12, 3), (18, 0)):
-            for s in range(PASSES):
-                for k, sort in enumerate(("codes", "bytes")):
-                    gather_steps.setdefault(first + (s if first == 5 else 2 * s + k), []).append((pc, s, sort))
+        for first, pc in GATHER_STEPS:
+            for k, what in enumerate(((0, "codes"), (1, "codes"), (0, "bytes"))):
+                gather_steps.setdefault(first + k // (2 if first == 5 else 1), []).append((pc, *what))
 
-        for i in range(RAW_BUFS):
-            load(i)
-        for i in range(total + 6):
+        step_of = {c[:3]: i for i, c in enumerate(chunks)}
+        for n, e in enumerate(ORDER):
+            i1, i3 = step_of[("w1", e, 1)], step_of[("w3", e, 1)]
+            later(i1 + 1, lambda e=e: first_products(e))
+            if e != ORDER[-1]:
+                later(i3 + 1, lambda e=e: second_products(e, 1))
+                later(i3 + 2, lambda e=e: sigmoids(e))
+                if n > 0:
+                    later(i3 + 2, lambda e=ORDER[n - 1]: project(e))
+                later(i3 + 2, lambda e=e: multiply(e, 1))
+                later(i3 + 3, lambda e=e: turn(e))
+            else:
+                later(i1 + 1, lambda e=e: sigmoids(e))
+                later(i1 + 1, lambda e=ORDER[n - 1]: project(e))
+                later(i3 + 1, lambda e=e: second_products(e, 2))
+                later(i3 + 1, lambda e=e: multiply(e, 2))
+                later(i3 + 1, lambda e=e: turn(e))
+                later(i3 + 1, lambda e=e: project(e))
+
+        nxt = 0
+        for i in range(total + 1):
             if i < total:
+                while nxt < len(chunks) and (nxt <= i or i == 0) and (chunks[nxt][0] == "w2" or room()):
+                    load(nxt)
+                    nxt += 1
                 interleave(i)
-            if i + RAW_BUFS < len(chunks):
-                load(i + RAW_BUFS)
-            if i == RAW_BUFS:
-                nc.sync.dma_start(pos1_t[:], pos1)
-                nc.sync.dma_start(pos2_t[:], pos2)
-            if 0 < i <= total:
+            if i > 0:
                 quantise(i - 1)
             for g in gather_steps.get(i, []):
                 gather(*g)
-            done = chunks[i - 1] if 0 < i <= total else ("none",)
-            if done[0] in ("w1", "w3") and done[2] == 1 and done[4] == H:
-                e = done[1]
-                lag = 0 if e == ORDER[-1] else 1
-                for u in range(COUNTS[e] // UNIT):
-                    if done[0] == "w1":
-                        later(i + lag * u, lambda e=e, u=u: gate_half(e, u))
-                    else:
-                        later(i + lag * u, lambda e=e, u=u, parts=1 if lag else 2: value_half(e, u, parts))
-                        later(i + lag * (u + 1), lambda e=e, u=u: turn(e, u))
-                        later(i + lag * (u + 2), lambda e=e, u=u: project(e, u))
-                if done[0] == "w3":
-                    later(i + lag * (COUNTS[e] // UNIT + 2), lambda e=e: leave(e))
             for task in tasks.get(i, []):
                 task()
+            while nxt < len(chunks) and nxt <= i + 14 and (chunks[nxt][0] == "w2" or room()):
+                load(nxt)
+                nxt += 1
+            if i == 8:
+                nc.sync.dma_start(pos1_t[:], pos1)
+                nc.sync.dma_start(pos2_t[:], pos2)
 
         o1 = keep.tile([P, T], F32, name="o1")
         nc.vector.tensor_tensor(o1[:], y[:].indirect(pos1_t[:]), gates[0][:], MULT)

@@ -18,8 +18,12 @@ PIECE = 384
 UNIT = 128
 V_CHUNKS = {3: (2, 3), 4: (2, 3), 5: (2, 3), 0: (2, 3), 1: (2, 3), 2: (1, 2)}
 RING = 9
-GRP_BUFS = 8
-GATHER_STEPS = ((5, 1), (7, 2), (10, 3), (13, 0))
+GRP_BUFS = 6
+FIRST_W = 2
+X_SPLIT = 256
+W2_ENGINE = "S"
+LAST_SPLIT = 160
+GATHER_STEPS = ((4, 1), (6, 2), (10, 3), (14, 0))
 
 F32 = mybir.dt.float32
 BF16 = mybir.dt.bfloat16
@@ -60,19 +64,19 @@ def tile_moe_rag_glu_sigmoid_kernel(tc, xT, w1, w3, w2, gate, offs, pos1, pos2, 
         nc.gpsimd.memset(x_bytes[:], 0)
         make_identity(nc, ident[:])
         nc.scalar.activation(warm[:], warm[:], SIGMOID)
-        nc.sync.dma_start(offs_t[:], offs)
 
         chunks = []
-        for s in range(PASSES):
-            chunks += [("x", s, 0, 256), ("x", s, 256, 768)]
         for e in ORDER:
-            chunks += [("w2", e)]
+            if e != ORDER[-1]:
+                chunks += [("w2", e)]
             for name in ("w1", "w3"):
                 for s in range(PASSES):
                     if (name, e, s) == ("w3", ORDER[-1], 1):
                         chunks += [(name, e, s, 0, 256), (name, e, s, 256, 512)]
                     else:
                         chunks += [(name, e, s, 0, 512)]
+        chunks += [("w2", ORDER[-1])]
+        chunks = chunks[1:FIRST_W] + [("x", 0, 0, T), ("x", 1, 0, T), chunks[0]] + chunks[FIRST_W:]
         total = len(chunks)
         chunks += [("gate", 0), ("gate", 1)]
 
@@ -114,9 +118,14 @@ def tile_moe_rag_glu_sigmoid_kernel(tc, xT, w1, w3, w2, gate, offs, pos1, pos2, 
                     k0, c0, c1 = c[2] * K_PASS, c[3], c[4]
                     w = w1 if c[0] == "w1" else w3
                     src = w[c[1], k0 : k0 + K_PASS, c0:c1]
-                raw, entry_of[i] = ring_tile([P, J, c1 - c0], F32)
+                if c[0] == "x":
+                    raw, entry_of[i] = keep.tile([P, J, T], F32, name=f"x_raw{c[1]}"), {}
+                else:
+                    raw, entry_of[i] = ring_tile([P, J, c1 - c0], F32)
                 nc.sync.dma_start(raw[:], src.rearrange("(p j) c -> p j c", j=J))
                 raw_of[i] = raw
+                if c[:2] == ("x", 1):
+                    nc.sync.dma_start(offs_t[:], offs)
 
         def interleave(i):
             c = chunks[i]
@@ -124,14 +133,18 @@ def tile_moe_rag_glu_sigmoid_kernel(tc, xT, w1, w3, w2, gate, offs, pos1, pos2, 
             if c[0] == "w2":
                 wide = N
                 grp = grps.tile([P, wide, J], BF16, name="grp2", align_bytes=64)
-                shares = [(0, wide, "V")]
+                shares = [(0, wide, W2_ENGINE)]
             else:
                 wide = c[-1] - c[-2]
-                grp = grps.tile([P, wide, J], BF16, name="grp", align_bytes=64)
                 if c[0] == "x":
-                    shares = [(0, wide, "V" if wide == 512 else "S")]
+                    grp = keep.tile([P, wide, J], BF16, name=f"x_grp{c[1]}", align_bytes=64)
+                    shares = [(0, X_SPLIT, "S"), (X_SPLIT, T, "V")]
+                else:
+                    grp = grps.tile([P, wide, J], BF16, name="grp", align_bytes=64)
+                if c[0] == "x":
+                    pass
                 elif wide == 256:
-                    shares = [(0, 160, "V"), (160, 256, "S")]
+                    shares = [(0, LAST_SPLIT, "V"), (LAST_SPLIT, 256, "S")]
                 else:
                     k = ("w1", "w3").index(c[0]) * 2 + c[2]
                     shares = [(0, wide, "V" if k in V_CHUNKS[c[1]] else "S")]
@@ -149,8 +162,9 @@ def tile_moe_rag_glu_sigmoid_kernel(tc, xT, w1, w3, w2, gate, offs, pos1, pos2, 
         def quantise(i):
             c = chunks[i]
             if c[0] == "x":
-                cols = slice(c[2], c[3])
-                nc.vector.quantize_mx(x_codes[c[1]][:, cols].bitcast(FP8X4), x_bytes[4 * c[1] : P, cols], grp_of[i])
+                for c0, c1 in ((0, 256), (256, T)):
+                    cols = slice(c0, c1)
+                    nc.vector.quantize_mx(x_codes[c[1]][:, cols].bitcast(FP8X4), x_bytes[4 * c[1] : P, cols], grp_of[i][:, J * c0 : J * c1])
                 return
             if c[0] == "w2":
                 cc = codes.tile([P, N], U32, name="w2_c", align_bytes=64)
@@ -244,7 +258,7 @@ def tile_moe_rag_glu_sigmoid_kernel(tc, xT, w1, w3, w2, gate, offs, pos1, pos2, 
 
         def turn(e):
             if e == ORDER[-1]:
-                ht = hid.tile([P, 3, UNIT, J], BF16, name="ht", align_bytes=64)
+                ht = keep.tile([P, 1, UNIT, J], BF16, name="ht", align_bytes=64)
                 entry = {}
             else:
                 ht, entry = ring_tile([P, len(units(e)), UNIT, J], BF16)
@@ -275,7 +289,7 @@ def tile_moe_rag_glu_sigmoid_kernel(tc, xT, w1, w3, w2, gate, offs, pos1, pos2, 
         gather_steps = {}
         for first, pc in GATHER_STEPS:
             for k, what in enumerate(((0, "codes"), (1, "codes"), (0, "bytes"))):
-                gather_steps.setdefault(first + k // (2 if first == 5 else 1), []).append((pc, *what))
+                gather_steps.setdefault(first + k // (2 if pc == 1 else 1), []).append((pc, *what))
 
         step_of = {c[:3]: i for i, c in enumerate(chunks)}
         for n, e in enumerate(ORDER):
@@ -294,7 +308,7 @@ def tile_moe_rag_glu_sigmoid_kernel(tc, xT, w1, w3, w2, gate, offs, pos1, pos2, 
                 later(i3 + 1, lambda e=e: second_products(e, 2))
                 later(i3 + 1, lambda e=e: multiply(e, 2))
                 later(i3 + 1, lambda e=e: turn(e))
-                later(i3 + 1, lambda e=e: project(e))
+                later(i3 + 2, lambda e=e: project(e))
 
         nxt = 0
         for i in range(total + 1):

from contextlib import ExitStack

import concourse.mybir as mybir
from concourse.masks import make_identity

T, E, H, N = 768, 6, 512, 128
SLOTS = 1536
STARTS = (0, 128, 256, 384, 768, 1152)
COUNTS = (128, 128, 128, 384, 384, 384)
ORDER = (3, 4, 5, 0, 1, 2)
FLOPS = 3422552064

P = 128
J = 4
K_PASS = 512
PASSES = 2
PIECE = 384
UNIT = 128
V_CHUNKS = {3: (2, 3), 4: (2, 3), 5: (2, 3), 0: (2, 3), 1: (2, 3), 2: (1, 2)}
RING = 9
GRP_BUFS = 6
FIRST_W = 2
X_SPLIT = 256
W2_ENGINE = "S"
LAST_SPLIT = 160
GATHER_STEPS = ((4, 1), (6, 2), (10, 3), (14, 0))

F32 = mybir.dt.float32
BF16 = mybir.dt.bfloat16
U32 = mybir.dt.uint32
U16 = mybir.dt.uint16
U8 = mybir.dt.uint8
FP8X4 = mybir.dt.float8_e4m3fn_x4
MULT = mybir.AluOpType.mult
ADD = mybir.AluOpType.add
SIGMOID = mybir.ActivationFunctionType.Sigmoid


def tile_moe_rag_glu_sigmoid_kernel(tc, xT, w1, w3, w2, gate, offs, pos1, pos2, out):
    nc = tc.nc
    with ExitStack() as ctx:
        lists = ctx.enter_context(tc.tile_pool(name="lists", bufs=1))
        keep = ctx.enter_context(tc.tile_pool(name="keep", bufs=1))
        raws = ctx.enter_context(tc.tile_pool(name="raws", bufs=1))
        raws2 = ctx.enter_context(tc.tile_pool(name="raws2", bufs=3))
        grps = ctx.enter_context(tc.tile_pool(name="grps", bufs=GRP_BUFS))
        codes = ctx.enter_context(tc.tile_pool(name="codes", bufs=3))
        slots = ctx.enter_context(tc.tile_pool(name="slots", bufs=2))
        hid = ctx.enter_context(tc.tile_pool(name="hid", bufs=6))
        psum_a = ctx.enter_context(tc.psum_pool(name="psum_a", bufs=1))
        psum_g = ctx.enter_context(tc.psum_pool(name="psum_g", bufs=1))
        psum_t = ctx.enter_context(tc.psum_pool(name="psum_t", bufs=2))

        offs_t = lists.tile([P, SLOTS // 16], U16, name="offs_t")
        pos1_t = lists.tile([P, T // 16], U16, name="pos1_t")
        pos2_t = lists.tile([P, T // 16], U16, name="pos2_t")
        y = keep.tile([P, SLOTS], F32, name="y")
        x_codes = [keep.tile([P, T], U32, name=f"x_codes{s}", align_bytes=64) for s in range(PASSES)]
        x_bytes = keep.tile([P, T], U8, name="x_bytes", align_bytes=64)
        ident = keep.tile([P, P], F32, name="ident")
        warm = keep.tile([P, 1], F32, name="warm")

        nc.gpsimd.memset(warm[:], 0.0)
        nc.gpsimd.memset(x_bytes[:], 0)
        make_identity(nc, ident[:])
        nc.scalar.activation(warm[:], warm[:], SIGMOID)

        chunks = []
        for e in ORDER:
            if e != ORDER[-1]:
                chunks += [("w2", e)]
            for name in ("w1", "w3"):
                for s in range(PASSES):
                    if (name, e, s) == ("w3", ORDER[-1], 1):
                        chunks += [(name, e, s, 0, 256), (name, e, s, 256, 512)]
                    else:
                        chunks += [(name, e, s, 0, 512)]
        chunks += [("w2", ORDER[-1])]
        chunks = chunks[1:FIRST_W] + [("x", 0, 0, T), ("x", 1, 0, T), chunks[0]] + chunks[FIRST_W:]
        total = len(chunks)
        chunks += [("gate", 0), ("gate", 1)]

        gates = []
        raw_of = {}
        grp_of = {}
        w_codes = {}
        w_bytes = {}

        ring = []

        def ring_tile(shape, dtype):
            n = len(ring)
            assert n < RING or ring[n - RING]["free"]
            tile = raws.tile(shape, dtype, name=f"ring{n % RING}", align_bytes=64)
            ring.append({"free": False})
            return tile, ring[-1]

        def room():
            return len(ring) < RING or ring[len(ring) - RING]["free"]

        entry_of = {}

        def load(i):
            c = chunks[i]
            if c[0] == "gate":
                raw, entry_of[i] = ring_tile([P, T], F32)
                nc.sync.dma_start(raw[:], gate[c[1]])
                gates.append(raw)
            elif c[0] == "w2":
                raw2 = raws2.tile([P, J, N], F32, name="raw2")
                nc.sync.dma_start(raw2[:], w2[c[1]].rearrange("(p j) n -> p j n", j=J))
                raw_of[i] = raw2
            else:
                if c[0] == "x":
                    k0, c0, c1 = c[1] * K_PASS, c[2], c[3]
                    src = xT[k0 : k0 + K_PASS, c0:c1]
                else:
                    k0, c0, c1 = c[2] * K_PASS, c[3], c[4]
                    w = w1 if c[0] == "w1" else w3
                    src = w[c[1], k0 : k0 + K_PASS, c0:c1]
                if c[0] == "x":
                    raw, entry_of[i] = keep.tile([P, J, T], F32, name=f"x_raw{c[1]}"), {}
                else:
                    raw, entry_of[i] = ring_tile([P, J, c1 - c0], F32)
                nc.sync.dma_start(raw[:], src.rearrange("(p j) c -> p j c", j=J))
                raw_of[i] = raw
                if c[:2] == ("x", 1):
                    nc.sync.dma_start(offs_t[:], offs)

        def interleave(i):
            c = chunks[i]
            raw = raw_of[i]
            if c[0] == "w2":
                wide = N
                grp = grps.tile([P, wide, J], BF16, name="grp2", align_bytes=64)
                shares = [(0, wide, W2_ENGINE)]
            else:
                wide = c[-1] - c[-2]
                if c[0] == "x":
                    grp = keep.tile([P, wide, J], BF16, name=f"x_grp{c[1]}", align_bytes=64)
                    shares = [(0, X_SPLIT, "S"), (X_SPLIT, T, "V")]
                else:
                    grp = grps.tile([P, wide, J], BF16, name="grp", align_bytes=64)
                if c[0] == "x":
                    pass
                elif wide == 256:
                    shares = [(0, LAST_SPLIT, "V"), (LAST_SPLIT, 256, "S")]
                else:
                    k = ("w1", "w3").index(c[0]) * 2 + c[2]
                    shares = [(0, wide, "V" if k in V_CHUNKS[c[1]] else "S")]
            for a, b, eng in shares:
                dst = grp[:, a:b, :].rearrange("p (c i) j -> p c j i", i=4)
                src = raw[:, :, a:b].rearrange("p j (c i) -> p c j i", i=4)
                if eng == "V":
                    nc.vector.tensor_copy(dst, src)
                else:
                    nc.scalar.copy(dst, src)
            grp_of[i] = grp[:].rearrange("p c j -> p (c j)")
            if c[0] != "w2":
                entry_of[i]["free"] = True

        def quantise(i):
            c = chunks[i]
            if c[0] == "x":
                for c0, c1 in ((0, 256), (256, T)):
                    cols = slice(c0, c1)
                    nc.vector.quantize_mx(x_codes[c[1]][:, cols].bitcast(FP8X4), x_bytes[4 * c[1] : P, cols], grp_of[i][:, J * c0 : J * c1])
                return
            if c[0] == "w2":
                cc = codes.tile([P, N], U32, name="w2_c", align_bytes=64)
                cb = codes.tile([P, N], U8, name="w2_b", align_bytes=64)
                w_codes[c], w_bytes[c] = cc, cb
                cols = slice(0, N)
            else:
                if c[3] == 0:
                    cc = codes.tile([P, H], U32, name=f"{c[0]}c{c[2]}", align_bytes=64)
                    cb = codes.tile([P, H], U8, name=f"{c[0]}b{c[2]}", align_bytes=64)
                    w_codes[c[:3]], w_bytes[c[:3]] = cc, cb
                cc, cb, cols = w_codes[c[:3]], w_bytes[c[:3]], slice(c[3], c[4])
            nc.vector.quantize_mx(cc[:, cols].bitcast(FP8X4), cb[:, cols], grp_of[i])

        def piece_of(e):
            return (0, e * UNIT) if e < 3 else (e - 2, 0)

        slot_codes = {}
        slot_bytes = {}

        def gather(pc, s, sort):
            if pc not in slot_codes:
                slot_codes[pc] = slots.tile([P, PASSES, PIECE], U32, name="sc", align_bytes=64)
                slot_bytes[pc] = slots.tile([P, PIECE], U8, name="sb", align_bytes=64)
            cols = offs_t[:, pc * (PIECE // 16) : (pc + 1) * (PIECE // 16)]
            if sort == "codes":
                nc.vector.tensor_copy(slot_codes[pc][:, s, :], x_codes[s][:].indirect(cols))
            else:
                nc.vector.tensor_copy(slot_bytes[pc][:], x_bytes[:].indirect(cols))

        def product(bank, name, e, u, c0, c1):
            pc, first = piece_of(e)
            mine = slice(first + u * UNIT, first + (u + 1) * UNIT)
            for s in range(PASSES):
                nc.tensor.matmul_mx(
                    bank[:, c0:c1],
                    lhsT=slot_codes[pc][:, s, mine].bitcast(FP8X4),
                    lhsT_scale=slot_bytes[pc][4 * s : P, mine],
                    rhs=w_codes[(name, e, s)][:, c0:c1].bitcast(FP8X4),
                    rhs_scale=w_bytes[(name, e, s)][:, c0:c1],
                    start=(s == 0),
                    stop=(s == PASSES - 1),
                )

        tasks = {}

        def later(step, task):
            tasks.setdefault(step, []).append(task)

        state = {}

        def units(e):
            return range(COUNTS[e] // UNIT)

        def first_products(e):
            for u in units(e):
                name = "ay" if u == units(e)[-1] else f"a{u}"
                a = psum_a.tile([P, H], F32, name=name)
                product(a, "w1", e, u, 0, H)
                state[("a", e, u)] = a

        def sigmoids(e):
            sg, state[("sg_entry", e)] = ring_tile([P, len(units(e)), H], F32)
            for u in units(e):
                nc.scalar.activation(sg[:, u, :], state[("a", e, u)][:], SIGMOID)
            state[("sg", e)] = sg

        def second_products(e, parts):
            wide = H // parts
            for u in units(e):
                g = psum_g.tile([P, H], F32, name=f"g{u}")
                for k in range(parts):
                    product(g, "w3", e, u, k * wide, (k + 1) * wide)
                state[("g", e, u)] = g

        def multiply(e, parts):
            wide = H // parts
            for u in units(e):
                h = hid.tile([P, H], BF16, name="h", align_bytes=64)
                for k in range(parts):
                    cols = slice(k * wide, (k + 1) * wide)
                    nc.vector.tensor_tensor(h[:, cols], state[("g", e, u)][:, cols], state[("sg", e)][:, u, cols], MULT)
                words = h[:].bitcast(F32)
                if u % 2 == 0:
                    tr = psum_t.tile([P, 4, UNIT], F32, name="tr")
                half = tr[:, 2 * (u % 2) : 2 * (u % 2) + 2, :]
                for k in range(2):
                    nc.tensor.transpose(half[:, k, :], words[:, k : 2 * UNIT : 2], ident[:])
                state[("tr", e, u)] = half
            state[("sg_entry", e)]["free"] = True

        def turn(e):
            if e == ORDER[-1]:
                ht = keep.tile([P, 1, UNIT, J], BF16, name="ht", align_bytes=64)
                entry = {}
            else:
                ht, entry = ring_tile([P, len(units(e)), UNIT, J], BF16)
            for u in units(e):
                nc.scalar.copy(ht[:, u, :, :].bitcast(F32), state[("tr", e, u)].rearrange("p k r -> p r k"))
            for u in units(e):
                hc = hid.tile([P, UNIT], U32, name="hc", align_bytes=64)
                hb = hid.tile([P, UNIT], U8, name="hb", align_bytes=64)
                nc.vector.quantize_mx(hc[:].bitcast(FP8X4), hb[:], ht[:, u, :, :].rearrange("p r j -> p (r j)"))
                state[("hc", e, u)] = (hc, hb)
            entry["free"] = True

        def project(e):
            yb = psum_a.tile([P, PIECE], F32, name="ay")
            for u in units(e):
                hc, hb = state[("hc", e, u)]
                nc.tensor.matmul_mx(
                    yb[:, u * UNIT : (u + 1) * UNIT],
                    lhsT=w_codes[("w2", e)][:].bitcast(FP8X4),
                    lhsT_scale=w_bytes[("w2", e)][:],
                    rhs=hc[:].bitcast(FP8X4),
                    rhs_scale=hb[:],
                    start=True,
                    stop=True,
                )
            nc.scalar.copy(y[:, STARTS[e] : STARTS[e] + COUNTS[e]], yb[:, : COUNTS[e]])

        gather_steps = {}
        for first, pc in GATHER_STEPS:
            for k, what in enumerate(((0, "codes"), (1, "codes"), (0, "bytes"))):
                gather_steps.setdefault(first + k // (2 if pc == 1 else 1), []).append((pc, *what))

        step_of = {c[:3]: i for i, c in enumerate(chunks)}
        for n, e in enumerate(ORDER):
            i1, i3 = step_of[("w1", e, 1)], step_of[("w3", e, 1)]
            later(i1 + 1, lambda e=e: first_products(e))
            if e != ORDER[-1]:
                later(i3 + 1, lambda e=e: second_products(e, 1))
                later(i3 + 2, lambda e=e: sigmoids(e))
                if n > 0:
                    later(i3 + 2, lambda e=ORDER[n - 1]: project(e))
                later(i3 + 2, lambda e=e: multiply(e, 1))
                later(i3 + 3, lambda e=e: turn(e))
            else:
                later(i1 + 1, lambda e=e: sigmoids(e))
                later(i1 + 1, lambda e=ORDER[n - 1]: project(e))
                later(i3 + 1, lambda e=e: second_products(e, 2))
                later(i3 + 1, lambda e=e: multiply(e, 2))
                later(i3 + 1, lambda e=e: turn(e))
                later(i3 + 2, lambda e=e: project(e))

        nxt = 0
        for i in range(total + 1):
            if i < total:
                while nxt < len(chunks) and (nxt <= i or i == 0) and (chunks[nxt][0] == "w2" or room()):
                    load(nxt)
                    nxt += 1
                interleave(i)
            if i > 0:
                quantise(i - 1)
            for g in gather_steps.get(i, []):
                gather(*g)
            for task in tasks.get(i, []):
                task()
            while nxt < len(chunks) and nxt <= i + 14 and (chunks[nxt][0] == "w2" or room()):
                load(nxt)
                nxt += 1
            if i == 8:
                nc.sync.dma_start(pos1_t[:], pos1)
                nc.sync.dma_start(pos2_t[:], pos2)

        o1 = keep.tile([P, T], F32, name="o1")
        nc.vector.tensor_tensor(o1[:], y[:].indirect(pos1_t[:]), gates[0][:], MULT)
        for half in range(2):
            cols = slice(half * PIECE, (half + 1) * PIECE)
            o2 = keep.tile([P, PIECE], F32, name=f"o2_{half}")
            total_out = keep.tile([P, PIECE], F32, name=f"total_out{half}")
            nc.vector.tensor_tensor(o2[:], y[:].indirect(pos2_t[:, half * 24 : (half + 1) * 24]), gates[1][:, cols], MULT)
            nc.vector.tensor_tensor(total_out[:], o1[:, cols], o2[:], ADD)
            nc.sync.dma_start(out[:, cols], total_out[:])
